import numpy as np, ml_dtypes
CORES = [100,101,102,103,108,109,110,111]
N = 8
NH, QP = 8, 128
def setup_inputs(rng):
    return {"q": rng.standard_normal((N, 128, NH * QP), dtype=np.float32).astype(ml_dtypes.bfloat16), "k": rng.standard_normal((N, 128, NH * 128), dtype=np.float32).astype(ml_dtypes.bfloat16), "v": rng.standard_normal((N, 128, NH * 128), dtype=np.float32).astype(ml_dtypes.bfloat16)}
def setup_inputs_big(rng):
    d = setup_inputs(rng)
    for k in ("q", "k", "v"): d[k] = (d[k].astype(np.float32) * 1024.0).astype(d[k].dtype)
    return d
def setup_inputs_small(rng):
    d = setup_inputs(rng)
    for k in ("q", "k", "v"): d[k] = (d[k].astype(np.float32) * (1 / 1024.0)).astype(d[k].dtype)
    return d
def setup_inputs_apart(rng):
    d = setup_inputs(rng)
    f = (10.0 ** rng.permutation(np.linspace(-1.5, 1.5, N))).astype(np.float32).reshape(N, 1, 1)
    for k in ("q", "k", "v"): d[k] = (d[k].astype(np.float32) * f).astype(d[k].dtype)
    return d
def reference(q, k, v):
    Q, K, V = q.astype(np.float64), k.astype(np.float64), v.astype(np.float64)
    y = np.zeros((N, 128, NH * QP))
    for r in range(N):
        for h in range(NH):
            for j in range(N):
                S = np.maximum(K[j][:, 128 * h:128 * h + 128].T @ Q[r][:, QP * h:QP * h + QP], 0.0)
                y[r][:, QP * h:QP * h + QP] += V[j][:, 128 * h:128 * h + 128].T @ S
    return {"y": y.astype(ml_dtypes.bfloat16 if q.dtype != np.float64 else np.float64)}

@@ -1,0 +1,262 @@
+from concourse.bass import DstId, RemoteDMATransfer
+from concourse.mybir import AluOpType
+
+NH, D, G = 8, 128, 4
+NHW = NH // G
+HELP = 0
+CH = 2
+LA = 2
+MERGE_DIRECT = True
+SPLIT_POOL = True
+W = NHW * D
+NQ = G * D
+UMAX = 2 * G * NHW
+NB = 8 - NHW
+
+BF = "bfloat16"
+SCRATCH = {
+    "qs": ("sbuf", [128, NH * D], BF), "ks": ("sbuf", [128, NH * D], BF), "vs": ("sbuf", [128, NH * D], BF),
+    "qland": ("sbuf", [128, G, W], BF),
+    "kl": ("sbuf", [128, 2 * G, W], BF), "vl": ("sbuf", [128, 2 * G, W], BF),
+    "rk": ("sbuf", [128, NH * D], BF), "rv": ("sbuf", [128, NH * D], BF),
+    "P": ("sbuf", [128, UMAX, NQ], BF), "zero": ("sbuf", [128, NQ], BF),
+    "part": ("sbuf", [128, NHW * NQ], BF), "pstage": ("sbuf", [128, NHW * NQ], BF),
+    "ystage": ("sbuf", [128, G, W], BF), "yland": ("sbuf", [128, NH * D], BF),
+}
+for _b in range(8):
+    SCRATCH["ps%d" % _b] = ("psum", [128, NQ], "float32")
+
+SEMAPHORES = (["ldk", "ldv", "ldq", "ldqo", "qin", "yin", "sent", "st", "own", "z"]
+              + ["kv%d" % s for s in range(2 * G)] + ["rl%d" % c for c in range(CH)]
+              + ["pin%d" % h for h in range(NHW)] + ["ev%d" % h for h in range(NHW)] + ["O%d" % h for h in range(NHW)]
+              + ["S%d" % u for u in range(UMAX)] + ["P%d" % u for u in range(UMAX)])
+
+
+def _bits(m):
+    return [b for b in range(m.bit_length()) if (m >> b) & 1]
+
+
+def _plan(T, topo):
+    cores = list(T.cores)
+    chips = []
+    for c in cores:
+        if topo.chip(c) not in chips:
+            chips.append(topo.chip(c))
+    allc = range(topo.CHIPS * topo.CORES_PER_CHIP)
+    ranks = [[c for c in cores if topo.chip(c) == ch] for ch in chips]
+    spare = [[c for c in allc if topo.chip(c) == ch and c not in cores] for ch in chips]
+    workers = []
+    for a in range(2):
+        ws = []
+        for d in range(G):
+            others = [j for j in range(G) if j != d]
+            given = others[:HELP]
+            ws.append(dict(core=ranks[a][d], h0=d * NHW, jl=[d] + others[HELP:], cross=True, sink=None,
+                           fed=bool(given)))
+            if given:
+                ws.append(dict(core=spare[a][d], h0=d * NHW, jl=given, cross=False, sink=ranks[a][d], fed=False))
+        workers.append(ws)
+
+    calls, expect, when = {}, {}, {}
+
+    def add(src, waits, trs, pool):
+        while trs:
+            n = min(len(trs), len(pool))
+            e = 1
+            while 2 * e * n <= len(pool):
+                e *= 2
+            out = []
+            for t, (dst, dap, sap, sem) in enumerate(trs[:n]):
+                out.append((dst, dap, sap, sem, sum(1 << b for b in pool[t * e:(t + 1) * e]), e))
+                expect[(dst, sem)] = expect.get((dst, sem), 0) + e
+            calls.setdefault(src, []).append((waits, out))
+            trs = trs[n:]
+
+    def cols(w):
+        return slice(w["h0"] * D, w["h0"] * D + W)
+
+    for a in range(2):
+        far0 = ranks[1 - a][0]
+        direct = [c for c in ranks[a] if topo.may_write(c, far0)]
+        indirect = [c for c in ranks[a] if c not in direct]
+        dies = [topo.die(c) for c in direct]
+        cand = sorted([h for h in spare[a] if topo.may_write(h, far0)], key=lambda h: (topo.die(h) in dies, h))
+        fw = sorted([w for w in workers[1 - a] if w["cross"]], key=lambda w: w["h0"])
+        per = len(fw) // CH
+        chunks = [fw[c * per:(c + 1) * per] for c in range(CH)]
+        for i, c in enumerate(ranks[a]):
+            near = _bits(topo.mask(c, [x for x in ranks[a] if x != c][0]))
+            slot = G + i
+            kvw = [("ldk", 16), ("ldv", 16)]
+            link = []
+            if c in direct:
+                rot = direct.index(c) % CH
+                farp = _bits(topo.mask(c, far0))
+                for p in range(CH):
+                    ci = (p + rot) % CH
+                    trs = []
+                    for w in chunks[ci]:
+                        trs.append((w["core"], T.kl[:, slot, :], T.ks[:, cols(w)], "kv%d" % slot))
+                        trs.append((w["core"], T.vl[:, slot, :], T.vs[:, cols(w)], "kv%d" % slot))
+                        when[(w["core"], slot)] = (2, p)
+                    link.append((c, kvw, trs, farp))
+                pool = [b for b in near if b not in farp] if SPLIT_POOL else near[::-1]
+            else:
+                n = indirect.index(c)
+                rot = n % CH
+                rel = cand[n]
+                farp = _bits(topo.mask(rel, far0))
+                for p in range(CH):
+                    ci = (p + rot) % CH
+                    cs = slice(chunks[ci][0]["h0"] * D, chunks[ci][-1]["h0"] * D + W)
+                    link.append((c, kvw, [(rel, T.rk[:, cs], T.ks[:, cs], "rl%d" % ci),
+                                          (rel, T.rv[:, cs], T.vs[:, cs], "rl%d" % ci)], near))
+                pool = near
+            qtr = [(w["core"], T.qland[:, i, :], T.qs[:, cols(w)], "qin") for w in workers[a] if w["core"] != c]
+            ktr = []
+            for w in workers[a]:
+                if i in w["jl"] and w["core"] != c:
+                    ktr.append((w["core"], T.kl[:, i, :], T.ks[:, cols(w)], "kv%d" % i))
+                    ktr.append((w["core"], T.vl[:, i, :], T.vs[:, cols(w)], "kv%d" % i))
+            head = link[:1] if c in direct else link
+            for x in head:
+                add(*x)
+            add(c, [("ldq", 16)], qtr, pool)
+            add(c, kvw, ktr, pool)
+            for x in link[len(head):]:
+                add(*x)
+            if c not in direct:
+                for p in range(CH):
+                    ci = (p + rot) % CH
+                    trs = []
+                    for w in chunks[ci]:
+                        trs.append((w["core"], T.kl[:, slot, :], T.rk[:, cols(w)], "kv%d" % slot))
+                        trs.append((w["core"], T.vl[:, slot, :], T.rv[:, cols(w)], "kv%d" % slot))
+                        when[(w["core"], slot)] = (3, p)
+                    add(rel, [("rl%d" % ci, None)], trs, farp)
+    for a in range(2):
+        for w in workers[a]:
+            c = w["core"]
+            near = _bits(topo.mask(c, [x for x in ranks[a] if x != c][0]))
+            if w["sink"] is None:
+                add(c, [("ev%d" % h, 1) for h in range(NHW)],
+                    [(rc, T.yland[:, cols(w)], T.ystage[:, r, :], "yin") for r, rc in enumerate(ranks[a]) if rc != c],
+                    near)
+            else:
+                for h in range(NHW):
+                    hs = slice(h * NQ, (h + 1) * NQ)
+                    add(c, [("ev%d" % h, 1)], [(w["sink"], T.part[:, hs], T.pstage[:, hs], "pin%d" % h)], near)
+    return ranks, workers, calls, expect, when
+
+
+def _compute(g, T, core, w, idx, expect, when):
+    tq, vq, sem = g.tensor, g.vector, T.sem
+    h0 = w["h0"]
+    srcs = [(0 if j == idx else 1, 0, j) for j in w["jl"]]
+    if w["cross"]:
+        srcs += [when[(core, G + i)] + (G + i,) for i in range(G)]
+    srcs.sort()
+    units, groups = [], []
+    if w["sink"] is not None:
+        for h in range(NHW):
+            for s in srcs:
+                units.append((s[2], h))
+        groups = [list(range(len(units)))]
+    else:
+        for s in srcs:
+            us = []
+            for h in range(NHW):
+                us.append(len(units))
+                units.append((s[2], h))
+            if groups and (s[0] < 2 or (s[0] == 2 and MERGE_DIRECT)):
+                groups[-1] += us
+            else:
+                groups.append(us)
+    seq = []
+    for grp in groups:
+        for t in range(len(grp) + LA):
+            if t < len(grp):
+                seq.append(("S", grp[t]))
+            if t >= LA:
+                seq.append(("O", grp[t - LA]))
+    vq.memset(T.zero[:, :], 0.0).then_inc(sem.z, 1)
+    vq.wait_ge(sem.z, 1)
+    tq.wait_ge(sem.qin, expect[(core, "qin")])
+    if idx is not None:
+        tq.wait_ge(sem.ldqo, 16)
+    seen, done, ns = [], [0] * NHW, len(srcs)
+    for kind, u in seq:
+        slot, h = units[u]
+        own = slot == idx
+        bank = T["ps%d" % (NHW + u % NB)]
+        acc = T["ps%d" % h]
+        hs = slice(h * D, (h + 1) * D)
+        gs = slice((h0 + h) * D, (h0 + h + 1) * D)
+        if kind == "S":
+            if slot not in seen:
+                seen.append(slot)
+                if own:
+                    tq.wait_ge(sem.ldk, 16)
+                    tq.wait_ge(sem.ldv, 16)
+                else:
+                    tq.wait_ge(sem["kv%d" % slot], expect[(core, "kv%d" % slot)])
+            tq.matmul(bank[:, :], T.ks[:, gs] if own else T.kl[:, slot, hs], T.qland[:, :, hs], True, True
+                      ).then_inc(sem["S%d" % u], 1)
+            vq.wait_ge(sem["S%d" % u], 1)
+            vq.tensor_tensor(T.P[:, u, :], bank[:, :], T.zero[:, :], AluOpType.max).then_inc(sem["P%d" % u], 1)
+        else:
+            tq.wait_ge(sem["P%d" % u], 1)
+            tq.matmul(acc[:, :], T.vs[:, gs] if own else T.vl[:, slot, hs], T.P[:, u, :], done[h] == 0,
+                      done[h] == ns - 1).then_inc(sem["O%d" % h], 1)
+            done[h] += 1
+            if done[h] == ns:
+                ps = slice(h * NQ, (h + 1) * NQ)
+                vq.wait_ge(sem["O%d" % h], ns)
+                if w["sink"] is not None:
+                    vq.tensor_copy(T.pstage[:, ps], acc[:, :]).then_inc(sem["ev%d" % h], 1)
+                elif w["fed"]:
+                    vq.wait_ge(sem["pin%d" % h], expect[(core, "pin%d" % h)])
+                    vq.tensor_tensor(T.ystage[:, :, hs], acc[:, :], T.part[:, ps], AluOpType.add
+                                     ).then_inc(sem["ev%d" % h], 1)
+                else:
+                    vq.tensor_copy(T.ystage[:, :, hs], acc[:, :]).then_inc(sem["ev%d" % h], 1)
+    if idx is not None and w["sink"] is None:
+        for h in range(NHW):
+            vq.wait_ge(sem["ev%d" % h], 1)
+        vq.tensor_copy(T.yland[:, h0 * D:h0 * D + W], T.ystage[:, idx, :]).then_inc(sem.own, 1)
+
+
+def rank_program(g, core, T, topo):
+    ranks, workers, calls, expect, when = _plan(T, topo)
+    sem = T.sem
+    mine = [w for ws in workers for w in ws if w["core"] == core]
+    idx = None
+    for rs in ranks:
+        if core in rs:
+            idx = rs.index(core)
+    if idx is not None:
+        g.sync.dma_start(T.ks[:, :], T.k[:, :]).then_inc(sem.ldk, 16)
+        g.scalar.dma_start(T.vs[:, :], T.v[:, :]).then_inc(sem.ldv, 16)
+        g.sync.dma_start(T.qs[:, :], T.q[:, :]).then_inc(sem.ldq, 16)
+        h0 = mine[0]["h0"]
+        g.scalar.dma_start(T.qland[:, idx, :], T.q[:, h0 * D:h0 * D + W]).then_inc(sem.ldqo, 16)
+    sent = 0
+    for waits, trs in calls.get(core, []):
+        for name, val in waits:
+            g.wait_ge(sem[name], expect[(core, name)] if val is None else val)
+        lst = []
+        for dst, dap, sap, name, m, e in trs:
+            rid, pid = topo.addr(dst)[:2]
+            lst.append(RemoteDMATransfer(dst_ids=[DstId(rid=rid, pnc=pid)], dma_engine_mask=m, remote_sem=sem[name],
+                                         src=sap, dst=dap))
+            sent += e
+        g.remote_dma_fused(lst, local_sem=sem.sent)
+    for w in mine:
+        _compute(g, T, core, w, idx, expect, when)
+    if sent:
+        g.wait_ge(sem.sent, sent)
+    if idx is not None:
+        g.sync.wait_ge(sem.yin, expect[(core, "yin")])
+        g.sync.wait_ge(sem.own, 1)
+        g.sync.dma_start(T.y[:, :], T.yland[:, :]).then_inc(sem.st, 16)
+        g.sync.wait_ge(sem.st, 16)

@@ -3,8 +3,10 @@ from concourse.mybir import AluOpType
 
 NH, D, G = 8, 128, 4
 NHW = NH // G
-HELP = 0
-CH = 2
+HELP = 3
+CH = 4
+SHIFT = 0
+HEADN = 2
 LA = 2
 MERGE_DIRECT = True
 SPLIT_POOL = True
@@ -12,13 +14,13 @@ W = NHW * D
 NQ = G * D
 UMAX = 2 * G * NHW
 NB = 8 - NHW
+PPC = G // CH
 
 BF = "bfloat16"
 SCRATCH = {
-    "qs": ("sbuf", [128, NH * D], BF), "ks": ("sbuf", [128, NH * D], BF), "vs": ("sbuf", [128, NH * D], BF),
-    "qland": ("sbuf", [128, G, W], BF),
-    "kl": ("sbuf", [128, 2 * G, W], BF), "vl": ("sbuf", [128, 2 * G, W], BF),
-    "rk": ("sbuf", [128, NH * D], BF), "rv": ("sbuf", [128, NH * D], BF),
+    "qs": ("sbuf", [128, NH * D], BF), "kvs": ("sbuf", [128, G, 2 * W], BF),
+    "qland": ("sbuf", [128, G, W], BF), "kvl": ("sbuf", [128, 2 * G, 2 * W], BF),
+    "rkv": ("sbuf", [128, G, 2 * W], BF),
     "P": ("sbuf", [128, UMAX, NQ], BF), "zero": ("sbuf", [128, NQ], BF),
     "part": ("sbuf", [128, NHW * NQ], BF), "pstage": ("sbuf", [128, NHW * NQ], BF),
     "ystage": ("sbuf", [128, G, W], BF), "yland": ("sbuf", [128, NH * D], BF),
@@ -26,7 +28,8 @@ SCRATCH = {
 for _b in range(8):
     SCRATCH["ps%d" % _b] = ("psum", [128, NQ], "float32")
 
-SEMAPHORES = (["ldk", "ldv", "ldq", "ldqo", "qin", "yin", "sent", "st", "own", "z"]
+SEMAPHORES = (["ldq", "ldqo", "qin", "yin", "sent", "st", "own", "z"]
+              + ["ldk%d" % c for c in range(CH)] + ["ldv%d" % c for c in range(CH)]
               + ["kv%d" % s for s in range(2 * G)] + ["rl%d" % c for c in range(CH)]
               + ["pin%d" % h for h in range(NHW)] + ["ev%d" % h for h in range(NHW)] + ["O%d" % h for h in range(NHW)]
               + ["S%d" % u for u in range(UMAX)] + ["P%d" % u for u in range(UMAX)])
@@ -34,6 +37,14 @@ SEMAPHORES = (["ldk", "ldv", "ldq", "ldqo", "qin", "yin", "sent", "st", "own", "
 
 def _bits(m):
     return [b for b in range(m.bit_length()) if (m >> b) & 1]
+
+
+def _loaded(cis):
+    return [("ldk%d" % ci, 16) for ci in cis] + [("ldv%d" % ci, 16) for ci in cis]
+
+
+def _pairs(ci):
+    return ci if PPC == 1 else slice(ci * PPC, (ci + 1) * PPC)
 
 
 def _plan(T, topo):
@@ -51,13 +62,12 @@ def _plan(T, topo):
         for d in range(G):
             others = [j for j in range(G) if j != d]
             given = others[:HELP]
-            ws.append(dict(core=ranks[a][d], h0=d * NHW, jl=[d] + others[HELP:], cross=True, sink=None,
-                           fed=bool(given)))
+            ws.append(dict(core=ranks[a][d], d=d, jl=[d] + others[HELP:], cross=True, sink=None, fed=bool(given)))
             if given:
-                ws.append(dict(core=spare[a][d], h0=d * NHW, jl=given, cross=False, sink=ranks[a][d], fed=False))
+                ws.append(dict(core=spare[a][d], d=d, jl=given, cross=False, sink=ranks[a][d], fed=False))
         workers.append(ws)
 
-    calls, expect, when = {}, {}, {}
+    calls, expect, when, rots = {}, {}, {}, {}
 
     def add(src, waits, trs, pool):
         while trs:
@@ -73,7 +83,7 @@ def _plan(T, topo):
             trs = trs[n:]
 
     def cols(w):
-        return slice(w["h0"] * D, w["h0"] * D + W)
+        return slice(w["d"] * W, (w["d"] + 1) * W)
 
     for a in range(2):
         far0 = ranks[1 - a][0]
@@ -81,59 +91,48 @@ def _plan(T, topo):
         indirect = [c for c in ranks[a] if c not in direct]
         dies = [topo.die(c) for c in direct]
         cand = sorted([h for h in spare[a] if topo.may_write(h, far0)], key=lambda h: (topo.die(h) in dies, h))
-        fw = sorted([w for w in workers[1 - a] if w["cross"]], key=lambda w: w["h0"])
-        per = len(fw) // CH
-        chunks = [fw[c * per:(c + 1) * per] for c in range(CH)]
+        fw = sorted([w for w in workers[1 - a] if w["cross"]], key=lambda w: w["d"])
+        chunks = [fw[c * PPC:(c + 1) * PPC] for c in range(CH)]
+        late = []
         for i, c in enumerate(ranks[a]):
             near = _bits(topo.mask(c, [x for x in ranks[a] if x != c][0]))
             slot = G + i
-            kvw = [("ldk", 16), ("ldv", 16)]
             link = []
-            if c in direct:
-                rot = direct.index(c) % CH
-                farp = _bits(topo.mask(c, far0))
-                for p in range(CH):
-                    ci = (p + rot) % CH
-                    trs = []
-                    for w in chunks[ci]:
-                        trs.append((w["core"], T.kl[:, slot, :], T.ks[:, cols(w)], "kv%d" % slot))
-                        trs.append((w["core"], T.vl[:, slot, :], T.vs[:, cols(w)], "kv%d" % slot))
-                        when[(w["core"], slot)] = (2, p)
-                    link.append((c, kvw, trs, farp))
-                pool = [b for b in near if b not in farp] if SPLIT_POOL else near[::-1]
+            n = direct.index(c) if c in direct else indirect.index(c)
+            rot = (n * CH // 2) % CH
+            rots[c] = rot
+            for p in range(CH):
+                ci = (p + rot) % CH
+                if c in direct:
+                    via, src = c, T.kvs
+                else:
+                    via, src = (direct[n] if p >= CH - SHIFT else cand[n]), T.rkv
+                    link.append((c, _loaded([ci]), [(via, T.rkv[:, _pairs(ci), :], T.kvs[:, _pairs(ci), :],
+                                                     "rl%d" % ci)], near))
+                farp = _bits(topo.mask(via, far0))
+                trs = []
+                for w in chunks[ci]:
+                    trs.append((w["core"], T.kvl[:, slot, :], src[:, w["d"], :], "kv%d" % slot))
+                    when[(w["core"], slot)] = (2 + p, 2) if c in direct else (4 + p, 3)
+                if c in direct:
+                    link.append((c, _loaded([ci]), trs, farp))
+                else:
+                    late.append((via, [("rl%d" % ci, None)], trs, farp))
+            if c in direct and SPLIT_POOL:
+                pool = [b for b in near if b not in farp]
             else:
-                n = indirect.index(c)
-                rot = n % CH
-                rel = cand[n]
-                farp = _bits(topo.mask(rel, far0))
-                for p in range(CH):
-                    ci = (p + rot) % CH
-                    cs = slice(chunks[ci][0]["h0"] * D, chunks[ci][-1]["h0"] * D + W)
-                    link.append((c, kvw, [(rel, T.rk[:, cs], T.ks[:, cs], "rl%d" % ci),
-                                          (rel, T.rv[:, cs], T.vs[:, cs], "rl%d" % ci)], near))
                 pool = near
             qtr = [(w["core"], T.qland[:, i, :], T.qs[:, cols(w)], "qin") for w in workers[a] if w["core"] != c]
-            ktr = []
-            for w in workers[a]:
-                if i in w["jl"] and w["core"] != c:
-                    ktr.append((w["core"], T.kl[:, i, :], T.ks[:, cols(w)], "kv%d" % i))
-                    ktr.append((w["core"], T.vl[:, i, :], T.vs[:, cols(w)], "kv%d" % i))
-            head = link[:1] if c in direct else link
-            for x in head:
+            ktr = [(w["core"], T.kvl[:, i, :], T.kvs[:, w["d"], :], "kv%d" % i)
+                   for w in workers[a] if i in w["jl"] and w["core"] != c]
+            for x in link[:HEADN]:
                 add(*x)
             add(c, [("ldq", 16)], qtr, pool)
-            add(c, kvw, ktr, pool)
-            for x in link[len(head):]:
+            add(c, _loaded(range(CH)), ktr, pool)
+            for x in link[HEADN:]:
                 add(*x)
-            if c not in direct:
-                for p in range(CH):
-                    ci = (p + rot) % CH
-                    trs = []
-                    for w in chunks[ci]:
-                        trs.append((w["core"], T.kl[:, slot, :], T.rk[:, cols(w)], "kv%d" % slot))
-                        trs.append((w["core"], T.vl[:, slot, :], T.rv[:, cols(w)], "kv%d" % slot))
-                        when[(w["core"], slot)] = (3, p)
-                    add(rel, [("rl%d" % ci, None)], trs, farp)
+        for x in late:
+            add(*x)
     for a in range(2):
         for w in workers[a]:
             c = w["core"]
@@ -146,13 +145,13 @@ def _plan(T, topo):
                 for h in range(NHW):
                     hs = slice(h * NQ, (h + 1) * NQ)
                     add(c, [("ev%d" % h, 1)], [(w["sink"], T.part[:, hs], T.pstage[:, hs], "pin%d" % h)], near)
-    return ranks, workers, calls, expect, when
+    return ranks, workers, calls, expect, when, rots
 
 
 def _compute(g, T, core, w, idx, expect, when):
     tq, vq, sem = g.tensor, g.vector, T.sem
-    h0 = w["h0"]
-    srcs = [(0 if j == idx else 1, 0, j) for j in w["jl"]]
+    d = w["d"]
+    srcs = [(0, 0, j) if j == idx else (1, 1, j) for j in w["jl"]]
     if w["cross"]:
         srcs += [when[(core, G + i)] + (G + i,) for i in range(G)]
     srcs.sort()
@@ -168,7 +167,7 @@ def _compute(g, T, core, w, idx, expect, when):
             for h in range(NHW):
                 us.append(len(units))
                 units.append((s[2], h))
-            if groups and (s[0] < 2 or (s[0] == 2 and MERGE_DIRECT)):
+            if groups and (s[1] < 2 or (s[1] == 2 and MERGE_DIRECT)):
                 groups[-1] += us
             else:
                 groups.append(us)
@@ -191,22 +190,22 @@ def _compute(g, T, core, w, idx, expect, when):
         bank = T["ps%d" % (NHW + u % NB)]
         acc = T["ps%d" % h]
         hs = slice(h * D, (h + 1) * D)
-        gs = slice((h0 + h) * D, (h0 + h + 1) * D)
+        vs = slice(W + h * D, W + (h + 1) * D)
         if kind == "S":
             if slot not in seen:
                 seen.append(slot)
                 if own:
-                    tq.wait_ge(sem.ldk, 16)
-                    tq.wait_ge(sem.ldv, 16)
+                    for name, val in _loaded([d // PPC]):
+                        tq.wait_ge(sem[name], val)
                 else:
                     tq.wait_ge(sem["kv%d" % slot], expect[(core, "kv%d" % slot)])
-            tq.matmul(bank[:, :], T.ks[:, gs] if own else T.kl[:, slot, hs], T.qland[:, :, hs], True, True
+            tq.matmul(bank[:, :], T.kvs[:, d, hs] if own else T.kvl[:, slot, hs], T.qland[:, :, hs], True, True
                       ).then_inc(sem["S%d" % u], 1)
             vq.wait_ge(sem["S%d" % u], 1)
             vq.tensor_tensor(T.P[:, u, :], bank[:, :], T.zero[:, :], AluOpType.max).then_inc(sem["P%d" % u], 1)
         else:
             tq.wait_ge(sem["P%d" % u], 1)
-            tq.matmul(acc[:, :], T.vs[:, gs] if own else T.vl[:, slot, hs], T.P[:, u, :], done[h] == 0,
+            tq.matmul(acc[:, :], T.kvs[:, d, vs] if own else T.kvl[:, slot, vs], T.P[:, u, :], done[h] == 0,
                       done[h] == ns - 1).then_inc(sem["O%d" % h], 1)
             done[h] += 1
             if done[h] == ns:
@@ -223,11 +222,11 @@ def _compute(g, T, core, w, idx, expect, when):
     if idx is not None and w["sink"] is None:
         for h in range(NHW):
             vq.wait_ge(sem["ev%d" % h], 1)
-        vq.tensor_copy(T.yland[:, h0 * D:h0 * D + W], T.ystage[:, idx, :]).then_inc(sem.own, 1)
+        vq.tensor_copy(T.yland[:, d * W:(d + 1) * W], T.ystage[:, idx, :]).then_inc(sem.own, 1)
 
 
 def rank_program(g, core, T, topo):
-    ranks, workers, calls, expect, when = _plan(T, topo)
+    ranks, workers, calls, expect, when, rots = _plan(T, topo)
     sem = T.sem
     mine = [w for ws in workers for w in ws if w["core"] == core]
     idx = None
@@ -235,11 +234,13 @@ def rank_program(g, core, T, topo):
         if core in rs:
             idx = rs.index(core)
     if idx is not None:
-        g.sync.dma_start(T.ks[:, :], T.k[:, :]).then_inc(sem.ldk, 16)
-        g.scalar.dma_start(T.vs[:, :], T.v[:, :]).then_inc(sem.ldv, 16)
+        for p in range(CH):
+            ci = (p + rots[core]) % CH
+            cs = slice(ci * PPC * W, (ci + 1) * PPC * W)
+            g.sync.dma_start(T.kvs[:, _pairs(ci), 0:W], T.k[:, cs]).then_inc(sem["ldk%d" % ci], 16)
+            g.scalar.dma_start(T.kvs[:, _pairs(ci), W:2 * W], T.v[:, cs]).then_inc(sem["ldv%d" % ci], 16)
         g.sync.dma_start(T.qs[:, :], T.q[:, :]).then_inc(sem.ldq, 16)
-        h0 = mine[0]["h0"]
-        g.scalar.dma_start(T.qland[:, idx, :], T.q[:, h0 * D:h0 * D + W]).then_inc(sem.ldqo, 16)
+        g.scalar.dma_start(T.qland[:, idx, :], T.q[:, idx * W:(idx + 1) * W]).then_inc(sem.ldqo, 16)
     sent = 0
     for waits, trs in calls.get(core, []):
         for name, val in waits:

@@ -15,6 +15,8 @@ NQ = G * D
 UMAX = 2 * G * NHW
 NB = 8 - NHW
 PPC = G // CH
+HR = G // 2
+HQ = HR * D
 
 BF = "bfloat16"
 SCRATCH = {
@@ -28,10 +30,12 @@ SCRATCH = {
 for _b in range(8):
     SCRATCH["ps%d" % _b] = ("psum", [128, NQ], "float32")
 
-SEMAPHORES = (["ldq", "ldqo", "qin", "yin", "sent", "st", "own", "z"]
+SEMAPHORES = (["ldq", "ldqo", "qin", "yinA", "yinB", "sent", "st", "stA", "own", "z", "evA", "evB"]
               + ["ldk%d" % c for c in range(CH)] + ["ldv%d" % c for c in range(CH)]
               + ["kv%d" % s for s in range(2 * G)] + ["rl%d" % c for c in range(CH)]
-              + ["pin%d" % h for h in range(NHW)] + ["ev%d" % h for h in range(NHW)] + ["O%d" % h for h in range(NHW)]
+              + ["pin%d" % h for h in range(NHW)] + ["ev%d" % h for h in range(NHW)]
+              + ["O%d" % b for b in range(2 * NHW)]
+              + ["SX%d" % i for i in range(2 * NHW)] + ["PX%d" % i for i in range(2 * NHW)]
               + ["S%d" % u for u in range(UMAX)] + ["P%d" % u for u in range(UMAX)])
 
 
@@ -138,9 +142,11 @@ def _plan(T, topo):
             c = w["core"]
             near = _bits(topo.mask(c, [x for x in ranks[a] if x != c][0]))
             if w["sink"] is None:
-                add(c, [("ev%d" % h, 1) for h in range(NHW)],
-                    [(rc, T.yland[:, cols(w)], T.ystage[:, r, :], "yin") for r, rc in enumerate(ranks[a]) if rc != c],
-                    near)
+                hb = w["d"] // HR
+                for name, land, half in (("evA", "yinA", 1 - hb), ("evB", "yinB", hb)):
+                    add(c, [(name, NHW)],
+                        [(rc, T.yland[:, cols(w)], T.ystage[:, r, :], land) for r, rc in enumerate(ranks[a])
+                         if rc != c and r // HR == half], near)
             else:
                 for h in range(NHW):
                     hs = slice(h * NQ, (h + 1) * NQ)
@@ -148,45 +154,22 @@ def _plan(T, topo):
     return ranks, workers, calls, expect, when, rots
 
 
-def _compute(g, T, core, w, idx, expect, when):
+def _spare(g, T, core, w, expect):
     tq, vq, sem = g.tensor, g.vector, T.sem
-    d = w["d"]
-    srcs = [(0, 0, j) if j == idx else (1, 1, j) for j in w["jl"]]
-    if w["cross"]:
-        srcs += [when[(core, G + i)] + (G + i,) for i in range(G)]
-    srcs.sort()
-    units, groups = [], []
-    if w["sink"] is not None:
-        for h in range(NHW):
-            for s in srcs:
-                units.append((s[2], h))
-        groups = [list(range(len(units)))]
-    else:
-        for s in srcs:
-            us = []
-            for h in range(NHW):
-                us.append(len(units))
-                units.append((s[2], h))
-            if groups and (s[1] < 2 or (s[1] == 2 and MERGE_DIRECT)):
-                groups[-1] += us
-            else:
-                groups.append(us)
+    units = [(j, h) for h in range(NHW) for j in sorted(w["jl"])]
+    ns = len(w["jl"])
     seq = []
-    for grp in groups:
-        for t in range(len(grp) + LA):
-            if t < len(grp):
-                seq.append(("S", grp[t]))
-            if t >= LA:
-                seq.append(("O", grp[t - LA]))
+    for t in range(len(units) + LA):
+        if t < len(units):
+            seq.append(("S", t))
+        if t >= LA:
+            seq.append(("O", t - LA))
     vq.memset(T.zero[:, :], 0.0).then_inc(sem.z, 1)
     vq.wait_ge(sem.z, 1)
     tq.wait_ge(sem.qin, expect[(core, "qin")])
-    if idx is not None:
-        tq.wait_ge(sem.ldqo, 16)
-    seen, done, ns = [], [0] * NHW, len(srcs)
+    seen, done = [], [0] * NHW
     for kind, u in seq:
         slot, h = units[u]
-        own = slot == idx
         bank = T["ps%d" % (NHW + u % NB)]
         acc = T["ps%d" % h]
         hs = slice(h * D, (h + 1) * D)
@@ -194,35 +177,120 @@ def _compute(g, T, core, w, idx, expect, when):
         if kind == "S":
             if slot not in seen:
                 seen.append(slot)
-                if own:
+                tq.wait_ge(sem["kv%d" % slot], expect[(core, "kv%d" % slot)])
+            tq.matmul(bank[:, :], T.kvl[:, slot, hs], T.qland[:, :, hs], True, True).then_inc(sem["S%d" % u], 1)
+            vq.wait_ge(sem["S%d" % u], 1)
+            vq.tensor_tensor(T.P[:, u, :], bank[:, :], T.zero[:, :], AluOpType.max).then_inc(sem["P%d" % u], 1)
+        else:
+            tq.wait_ge(sem["P%d" % u], 1)
+            tq.matmul(acc[:, :], T.kvl[:, slot, vs], T.P[:, u, :], done[h] == 0, done[h] == ns - 1
+                      ).then_inc(sem["O%d" % h], 1)
+            done[h] += 1
+            if done[h] == ns:
+                vq.wait_ge(sem["O%d" % h], ns)
+                vq.tensor_copy(T.pstage[:, h * NQ:(h + 1) * NQ], acc[:, :]).then_inc(sem["ev%d" % h], 1)
+
+
+def _worker(g, T, core, w, idx, expect, when):
+    tq, vq, sem = g.tensor, g.vector, T.sem
+    d = w["d"]
+    hb = d // HR
+    ha = 1 - hb
+    srcs = [(0, 0, j) if j == idx else (1, 1, j) for j in w["jl"]]
+    srcs += [when[(core, G + i)] + (G + i,) for i in range(G)]
+    srcs.sort()
+    ns = len(srcs)
+    units, groups = [], []
+    for s in srcs[:-1]:
+        us = []
+        for h in range(NHW):
+            us.append(len(units))
+            units.append((s[2], h))
+        if groups and (s[1] < 2 or (s[1] == 2 and MERGE_DIRECT)):
+            groups[-1] += us
+        else:
+            groups.append(us)
+    seq = []
+    for grp in groups:
+        for t in range(len(grp) + LA):
+            if t < len(grp):
+                seq.append(("S", grp[t]))
+            if t >= LA:
+                seq.append(("O", grp[t - LA]))
+
+    def kblk(slot, h):
+        hs = slice(h * D, (h + 1) * D)
+        return T.kvs[:, d, hs] if slot == idx else T.kvl[:, slot, hs]
+
+    def vblk(slot, h):
+        vs = slice(W + h * D, W + (h + 1) * D)
+        return T.kvs[:, d, vs] if slot == idx else T.kvl[:, slot, vs]
+
+    def acc(h, half):
+        return T["ps%d" % (2 * h + half)]
+
+    def osem(h, half):
+        return sem["O%d" % (2 * h + half)]
+
+    nacc = 2 * NHW
+    nsb = 8 - nacc
+    vq.memset(T.zero[:, :], 0.0).then_inc(sem.z, 1)
+    vq.wait_ge(sem.z, 1)
+    tq.wait_ge(sem.qin, expect[(core, "qin")])
+    tq.wait_ge(sem.ldqo, 16)
+    seen, done = [], [0] * NHW
+    for kind, u in seq:
+        slot, h = units[u]
+        bank = T["ps%d" % (nacc + u % nsb)]
+        if kind == "S":
+            if slot not in seen:
+                seen.append(slot)
+                if slot == idx:
                     for name, val in _loaded([d // PPC]):
                         tq.wait_ge(sem[name], val)
                 else:
                     tq.wait_ge(sem["kv%d" % slot], expect[(core, "kv%d" % slot)])
-            tq.matmul(bank[:, :], T.kvs[:, d, hs] if own else T.kvl[:, slot, hs], T.qland[:, :, hs], True, True
+            tq.matmul(bank[:, :], kblk(slot, h), T.qland[:, :, h * D:(h + 1) * D], True, True
                       ).then_inc(sem["S%d" % u], 1)
             vq.wait_ge(sem["S%d" % u], 1)
             vq.tensor_tensor(T.P[:, u, :], bank[:, :], T.zero[:, :], AluOpType.max).then_inc(sem["P%d" % u], 1)
         else:
             tq.wait_ge(sem["P%d" % u], 1)
-            tq.matmul(acc[:, :], T.kvs[:, d, vs] if own else T.kvl[:, slot, vs], T.P[:, u, :], done[h] == 0,
-                      done[h] == ns - 1).then_inc(sem["O%d" % h], 1)
+            for half in (ha, hb):
+                tq.matmul(acc(h, half)[:, 0:HQ], vblk(slot, h), T.P[:, u, half * HQ:(half + 1) * HQ], done[h] == 0,
+                          False).then_inc(osem(h, half), 1)
             done[h] += 1
-            if done[h] == ns:
-                ps = slice(h * NQ, (h + 1) * NQ)
-                vq.wait_ge(sem["O%d" % h], ns)
-                if w["sink"] is not None:
-                    vq.tensor_copy(T.pstage[:, ps], acc[:, :]).then_inc(sem["ev%d" % h], 1)
-                elif w["fed"]:
-                    vq.wait_ge(sem["pin%d" % h], expect[(core, "pin%d" % h)])
-                    vq.tensor_tensor(T.ystage[:, :, hs], acc[:, :], T.part[:, ps], AluOpType.add
-                                     ).then_inc(sem["ev%d" % h], 1)
-                else:
-                    vq.tensor_copy(T.ystage[:, :, hs], acc[:, :]).then_inc(sem["ev%d" % h], 1)
-    if idx is not None and w["sink"] is None:
-        for h in range(NHW):
-            vq.wait_ge(sem["ev%d" % h], 1)
-        vq.tensor_copy(T.yland[:, d * W:(d + 1) * W], T.ystage[:, idx, :]).then_inc(sem.own, 1)
+    slot = srcs[-1][2]
+    u0 = len(units)
+    hu = [(h, half) for half in (ha, hb) for h in range(NHW)]
+    tq.wait_ge(sem["kv%d" % slot], expect[(core, "kv%d" % slot)])
+    for i, (h, half) in enumerate(hu):
+        bank = T["ps%d" % (nacc + i)]
+        tq.matmul(bank[:, 0:HQ], kblk(slot, h), T.qland[:, half * HR:(half + 1) * HR, h * D:(h + 1) * D], True, True
+                  ).then_inc(sem["SX%d" % i], 1)
+        vq.wait_ge(sem["SX%d" % i], 1)
+        vq.tensor_tensor(T.P[:, u0 + h, half * HQ:(half + 1) * HQ], bank[:, 0:HQ], T.zero[:, 0:HQ], AluOpType.max
+                         ).then_inc(sem["PX%d" % i], 1)
+    for i, (h, half) in enumerate(hu):
+        tq.wait_ge(sem["PX%d" % i], 1)
+        tq.matmul(acc(h, half)[:, 0:HQ], vblk(slot, h), T.P[:, u0 + h, half * HQ:(half + 1) * HQ], False, True
+                  ).then_inc(osem(h, half), 1)
+
+    def out(dst, h, half, c0, n, name):
+        p0 = h * NQ + half * HQ + c0
+        vq.tensor_tensor(dst, acc(h, half)[:, c0:c0 + n], T.part[:, p0:p0 + n], AluOpType.add).then_inc(sem[name], 1)
+
+    for h in range(NHW):
+        vq.wait_ge(osem(h, ha), ns)
+        vq.wait_ge(sem["pin%d" % h], expect[(core, "pin%d" % h)])
+        out(T.ystage[:, ha * HR:(ha + 1) * HR, h * D:(h + 1) * D], h, ha, 0, HQ, "evA")
+    for h in range(NHW):
+        vq.wait_ge(osem(h, hb), ns)
+        for r in range(hb * HR, (hb + 1) * HR):
+            if r != d:
+                out(T.ystage[:, r, h * D:(h + 1) * D], h, hb, (r - hb * HR) * D, D, "evB")
+    for h in range(NHW):
+        out(T.yland[:, d * W + h * D:d * W + (h + 1) * D], h, hb, (d - hb * HR) * D, D, "own")
 
 
 def rank_program(g, core, T, topo):
@@ -239,8 +307,9 @@ def rank_program(g, core, T, topo):
             cs = slice(ci * PPC * W, (ci + 1) * PPC * W)
             g.sync.dma_start(T.kvs[:, _pairs(ci), 0:W], T.k[:, cs]).then_inc(sem["ldk%d" % ci], 16)
             g.scalar.dma_start(T.kvs[:, _pairs(ci), W:2 * W], T.v[:, cs]).then_inc(sem["ldv%d" % ci], 16)
-        g.sync.dma_start(T.qs[:, :], T.q[:, :]).then_inc(sem.ldq, 16)
-        g.scalar.dma_start(T.qland[:, idx, :], T.q[:, idx * W:(idx + 1) * W]).then_inc(sem.ldqo, 16)
+            if p == HEADN - 1:
+                g.sync.dma_start(T.qs[:, :], T.q[:, :]).then_inc(sem.ldq, 16)
+                g.scalar.dma_start(T.qland[:, idx, :], T.q[:, idx * W:(idx + 1) * W]).then_inc(sem.ldqo, 16)
     sent = 0
     for waits, trs in calls.get(core, []):
         for name, val in waits:
@@ -253,11 +322,20 @@ def rank_program(g, core, T, topo):
             sent += e
         g.remote_dma_fused(lst, local_sem=sem.sent)
     for w in mine:
-        _compute(g, T, core, w, idx, expect, when)
+        if w["sink"] is None:
+            _worker(g, T, core, w, idx, expect, when)
+        else:
+            _spare(g, T, core, w, expect)
     if sent:
         g.wait_ge(sem.sent, sent)
     if idx is not None:
-        g.sync.wait_ge(sem.yin, expect[(core, "yin")])
-        g.sync.wait_ge(sem.own, 1)
-        g.sync.dma_start(T.y[:, :], T.yland[:, :]).then_inc(sem.st, 16)
+        hb = idx // HR
+        ca = slice((1 - hb) * HR * W, (2 - hb) * HR * W)
+        cb = slice(hb * HR * W, (hb + 1) * HR * W)
+        g.scalar.wait_ge(sem.yinA, expect[(core, "yinA")])
+        g.scalar.dma_start(T.y[:, ca], T.yland[:, ca]).then_inc(sem.stA, 16)
+        g.scalar.wait_ge(sem.stA, 16)
+        g.sync.wait_ge(sem.yinB, expect[(core, "yinB")])
+        g.sync.wait_ge(sem.own, NHW)
+        g.sync.dma_start(T.y[:, cb], T.yland[:, cb]).then_inc(sem.st, 16)
         g.sync.wait_ge(sem.st, 16)

from concourse.bass import DstId, RemoteDMATransfer
from concourse.mybir import AluOpType

NH, D, G = 8, 128, 4
NHW = NH // G
HELP = 3
CH = 4
SHIFT = 0
HEADN = 2
LA = 2
MERGE_DIRECT = True
SPLIT_POOL = True
W = NHW * D
NQ = G * D
UMAX = 2 * G * NHW
NB = 8 - NHW
PPC = G // CH
HR = G // 2
HQ = HR * D

BF = "bfloat16"
SCRATCH = {
    "qs": ("sbuf", [128, NH * D], BF), "kvs": ("sbuf", [128, G, 2 * W], BF),
    "qland": ("sbuf", [128, G, W], BF), "kvl": ("sbuf", [128, 2 * G, 2 * W], BF),
    "rkv": ("sbuf", [128, G, 2 * W], BF),
    "P": ("sbuf", [128, UMAX, NQ], BF), "zero": ("sbuf", [128, NQ], BF),
    "part": ("sbuf", [128, NHW * NQ], BF), "pstage": ("sbuf", [128, NHW * NQ], BF),
    "ystage": ("sbuf", [128, G, W], BF), "yland": ("sbuf", [128, NH * D], BF),
}
for _b in range(8):
    SCRATCH["ps%d" % _b] = ("psum", [128, NQ], "float32")

SEMAPHORES = (["ldq", "ldqo", "qin", "yinA", "yinB", "sent", "st", "stA", "own", "z", "evA", "evB"]
              + ["ldk%d" % c for c in range(CH)] + ["ldv%d" % c for c in range(CH)]
              + ["kv%d" % s for s in range(2 * G)] + ["rl%d" % c for c in range(CH)]
              + ["pin%d" % h for h in range(NHW)] + ["ev%d" % h for h in range(NHW)]
              + ["O%d" % b for b in range(2 * NHW)]
              + ["SX%d" % i for i in range(2 * NHW)] + ["PX%d" % i for i in range(2 * NHW)]
              + ["S%d" % u for u in range(UMAX)] + ["P%d" % u for u in range(UMAX)])


def _bits(m):
    return [b for b in range(m.bit_length()) if (m >> b) & 1]


def _loaded(cis):
    return [("ldk%d" % ci, 16) for ci in cis] + [("ldv%d" % ci, 16) for ci in cis]


def _pairs(ci):
    return ci if PPC == 1 else slice(ci * PPC, (ci + 1) * PPC)


def _plan(T, topo):
    cores = list(T.cores)
    chips = []
    for c in cores:
        if topo.chip(c) not in chips:
            chips.append(topo.chip(c))
    allc = range(topo.CHIPS * topo.CORES_PER_CHIP)
    ranks = [[c for c in cores if topo.chip(c) == ch] for ch in chips]
    spare = [[c for c in allc if topo.chip(c) == ch and c not in cores] for ch in chips]
    workers = []
    for a in range(2):
        ws = []
        for d in range(G):
            others = [j for j in range(G) if j != d]
            given = others[:HELP]
            ws.append(dict(core=ranks[a][d], d=d, jl=[d] + others[HELP:], cross=True, sink=None, fed=bool(given)))
            if given:
                ws.append(dict(core=spare[a][d], d=d, jl=given, cross=False, sink=ranks[a][d], fed=False))
        workers.append(ws)

    calls, expect, when, rots = {}, {}, {}, {}

    def add(src, waits, trs, pool):
        while trs:
            n = min(len(trs), len(pool))
            e = 1
            while 2 * e * n <= len(pool):
                e *= 2
            out = []
            for t, (dst, dap, sap, sem) in enumerate(trs[:n]):
                out.append((dst, dap, sap, sem, sum(1 << b for b in pool[t * e:(t + 1) * e]), e))
                expect[(dst, sem)] = expect.get((dst, sem), 0) + e
            calls.setdefault(src, []).append((waits, out))
            trs = trs[n:]

    def cols(w):
        return slice(w["d"] * W, (w["d"] + 1) * W)

    for a in range(2):
        far0 = ranks[1 - a][0]
        direct = [c for c in ranks[a] if topo.may_write(c, far0)]
        indirect = [c for c in ranks[a] if c not in direct]
        dies = [topo.die(c) for c in direct]
        cand = sorted([h for h in spare[a] if topo.may_write(h, far0)], key=lambda h: (topo.die(h) in dies, h))
        fw = sorted([w for w in workers[1 - a] if w["cross"]], key=lambda w: w["d"])
        chunks = [fw[c * PPC:(c + 1) * PPC] for c in range(CH)]
        late = []
        for i, c in enumerate(ranks[a]):
            near = _bits(topo.mask(c, [x for x in ranks[a] if x != c][0]))
            slot = G + i
            link = []
            n = direct.index(c) if c in direct else indirect.index(c)
            rot = (n * CH // 2) % CH
            rots[c] = rot
            for p in range(CH):
                ci = (p + rot) % CH
                if c in direct:
                    via, src = c, T.kvs
                else:
                    via, src = (direct[n] if p >= CH - SHIFT else cand[n]), T.rkv
                    link.append((c, _loaded([ci]), [(via, T.rkv[:, _pairs(ci), :], T.kvs[:, _pairs(ci), :],
                                                     "rl%d" % ci)], near))
                farp = _bits(topo.mask(via, far0))
                trs = []
                for w in chunks[ci]:
                    trs.append((w["core"], T.kvl[:, slot, :], src[:, w["d"], :], "kv%d" % slot))
                    when[(w["core"], slot)] = (2 + p, 2) if c in direct else (4 + p, 3)
                if c in direct:
                    link.append((c, _loaded([ci]), trs, farp))
                else:
                    late.append((via, [("rl%d" % ci, None)], trs, farp))
            if c in direct and SPLIT_POOL:
                pool = [b for b in near if b not in farp]
            else:
                pool = near
            qtr = [(w["core"], T.qland[:, i, :], T.qs[:, cols(w)], "qin") for w in workers[a] if w["core"] != c]
            ktr = [(w["core"], T.kvl[:, i, :], T.kvs[:, w["d"], :], "kv%d" % i)
                   for w in workers[a] if i in w["jl"] and w["core"] != c]
            for x in link[:HEADN]:
                add(*x)
            add(c, [("ldq", 16)], qtr, pool)
            add(c, _loaded(range(CH)), ktr, pool)
            for x in link[HEADN:]:
                add(*x)
        for x in late:
            add(*x)
    for a in range(2):
        for w in workers[a]:
            c = w["core"]
            near = _bits(topo.mask(c, [x for x in ranks[a] if x != c][0]))
            if w["sink"] is None:
                hb = w["d"] // HR
                for name, land, half in (("evA", "yinA", 1 - hb), ("evB", "yinB", hb)):
                    add(c, [(name, NHW)],
                        [(rc, T.yland[:, cols(w)], T.ystage[:, r, :], land) for r, rc in enumerate(ranks[a])
                         if rc != c and r // HR == half], near)
            else:
                for h in range(NHW):
                    hs = slice(h * NQ, (h + 1) * NQ)
                    add(c, [("ev%d" % h, 1)], [(w["sink"], T.part[:, hs], T.pstage[:, hs], "pin%d" % h)], near)
    return ranks, workers, calls, expect, when, rots


def _spare(g, T, core, w, expect):
    tq, vq, sem = g.tensor, g.vector, T.sem
    units = [(j, h) for h in range(NHW) for j in sorted(w["jl"])]
    ns = len(w["jl"])
    seq = []
    for t in range(len(units) + LA):
        if t < len(units):
            seq.append(("S", t))
        if t >= LA:
            seq.append(("O", t - LA))
    vq.memset(T.zero[:, :], 0.0).then_inc(sem.z, 1)
    vq.wait_ge(sem.z, 1)
    tq.wait_ge(sem.qin, expect[(core, "qin")])
    seen, done = [], [0] * NHW
    for kind, u in seq:
        slot, h = units[u]
        bank = T["ps%d" % (NHW + u % NB)]
        acc = T["ps%d" % h]
        hs = slice(h * D, (h + 1) * D)
        vs = slice(W + h * D, W + (h + 1) * D)
        if kind == "S":
            if slot not in seen:
                seen.append(slot)
                tq.wait_ge(sem["kv%d" % slot], expect[(core, "kv%d" % slot)])
            tq.matmul(bank[:, :], T.kvl[:, slot, hs], T.qland[:, :, hs], True, True).then_inc(sem["S%d" % u], 1)
            vq.wait_ge(sem["S%d" % u], 1)
            vq.tensor_tensor(T.P[:, u, :], bank[:, :], T.zero[:, :], AluOpType.max).then_inc(sem["P%d" % u], 1)
        else:
            tq.wait_ge(sem["P%d" % u], 1)
            tq.matmul(acc[:, :], T.kvl[:, slot, vs], T.P[:, u, :], done[h] == 0, done[h] == ns - 1
                      ).then_inc(sem["O%d" % h], 1)
            done[h] += 1
            if done[h] == ns:
                vq.wait_ge(sem["O%d" % h], ns)
                vq.tensor_copy(T.pstage[:, h * NQ:(h + 1) * NQ], acc[:, :]).then_inc(sem["ev%d" % h], 1)


def _worker(g, T, core, w, idx, expect, when):
    tq, vq, sem = g.tensor, g.vector, T.sem
    d = w["d"]
    hb = d // HR
    ha = 1 - hb
    srcs = [(0, 0, j) if j == idx else (1, 1, j) for j in w["jl"]]
    srcs += [when[(core, G + i)] + (G + i,) for i in range(G)]
    srcs.sort()
    ns = len(srcs)
    units, groups = [], []
    for s in srcs[:-1]:
        us = []
        for h in range(NHW):
            us.append(len(units))
            units.append((s[2], h))
        if groups and (s[1] < 2 or (s[1] == 2 and MERGE_DIRECT)):
            groups[-1] += us
        else:
            groups.append(us)
    seq = []
    for grp in groups:
        for t in range(len(grp) + LA):
            if t < len(grp):
                seq.append(("S", grp[t]))
            if t >= LA:
                seq.append(("O", grp[t - LA]))

    def kblk(slot, h):
        hs = slice(h * D, (h + 1) * D)
        return T.kvs[:, d, hs] if slot == idx else T.kvl[:, slot, hs]

    def vblk(slot, h):
        vs = slice(W + h * D, W + (h + 1) * D)
        return T.kvs[:, d, vs] if slot == idx else T.kvl[:, slot, vs]

    def acc(h, half):
        return T["ps%d" % (2 * h + half)]

    def osem(h, half):
        return sem["O%d" % (2 * h + half)]

    nacc = 2 * NHW
    nsb = 8 - nacc
    vq.memset(T.zero[:, :], 0.0).then_inc(sem.z, 1)
    vq.wait_ge(sem.z, 1)
    tq.wait_ge(sem.qin, expect[(core, "qin")])
    tq.wait_ge(sem.ldqo, 16)
    seen, done = [], [0] * NHW
    for kind, u in seq:
        slot, h = units[u]
        bank = T["ps%d" % (nacc + u % nsb)]
        if kind == "S":
            if slot not in seen:
                seen.append(slot)
                if slot == idx:
                    for name, val in _loaded([d // PPC]):
                        tq.wait_ge(sem[name], val)
                else:
                    tq.wait_ge(sem["kv%d" % slot], expect[(core, "kv%d" % slot)])
            tq.matmul(bank[:, :], kblk(slot, h), T.qland[:, :, h * D:(h + 1) * D], True, True
                      ).then_inc(sem["S%d" % u], 1)
            vq.wait_ge(sem["S%d" % u], 1)
            vq.tensor_tensor(T.P[:, u, :], bank[:, :], T.zero[:, :], AluOpType.max).then_inc(sem["P%d" % u], 1)
        else:
            tq.wait_ge(sem["P%d" % u], 1)
            for half in (ha, hb):
                tq.matmul(acc(h, half)[:, 0:HQ], vblk(slot, h), T.P[:, u, half * HQ:(half + 1) * HQ], done[h] == 0,
                          False).then_inc(osem(h, half), 1)
            done[h] += 1
    slot = srcs[-1][2]
    u0 = len(units)
    hu = [(h, half) for half in (ha, hb) for h in range(NHW)]
    tq.wait_ge(sem["kv%d" % slot], expect[(core, "kv%d" % slot)])
    for i, (h, half) in enumerate(hu):
        bank = T["ps%d" % (nacc + i)]
        tq.matmul(bank[:, 0:HQ], kblk(slot, h), T.qland[:, half * HR:(half + 1) * HR, h * D:(h + 1) * D], True, True
                  ).then_inc(sem["SX%d" % i], 1)
        vq.wait_ge(sem["SX%d" % i], 1)
        vq.tensor_tensor(T.P[:, u0 + h, half * HQ:(half + 1) * HQ], bank[:, 0:HQ], T.zero[:, 0:HQ], AluOpType.max
                         ).then_inc(sem["PX%d" % i], 1)
    for i, (h, half) in enumerate(hu):
        tq.wait_ge(sem["PX%d" % i], 1)
        tq.matmul(acc(h, half)[:, 0:HQ], vblk(slot, h), T.P[:, u0 + h, half * HQ:(half + 1) * HQ], False, True
                  ).then_inc(osem(h, half), 1)

    def out(dst, h, half, c0, n, name):
        p0 = h * NQ + half * HQ + c0
        vq.tensor_tensor(dst, acc(h, half)[:, c0:c0 + n], T.part[:, p0:p0 + n], AluOpType.add).then_inc(sem[name], 1)

    for h in range(NHW):
        vq.wait_ge(osem(h, ha), ns)
        vq.wait_ge(sem["pin%d" % h], expect[(core, "pin%d" % h)])
        out(T.ystage[:, ha * HR:(ha + 1) * HR, h * D:(h + 1) * D], h, ha, 0, HQ, "evA")
    for h in range(NHW):
        vq.wait_ge(osem(h, hb), ns)
        for r in range(hb * HR, (hb + 1) * HR):
            if r != d:
                out(T.ystage[:, r, h * D:(h + 1) * D], h, hb, (r - hb * HR) * D, D, "evB")
    for h in range(NHW):
        out(T.yland[:, d * W + h * D:d * W + (h + 1) * D], h, hb, (d - hb * HR) * D, D, "own")


def rank_program(g, core, T, topo):
    ranks, workers, calls, expect, when, rots = _plan(T, topo)
    sem = T.sem
    mine = [w for ws in workers for w in ws if w["core"] == core]
    idx = None
    for rs in ranks:
        if core in rs:
            idx = rs.index(core)
    if idx is not None:
        for p in range(CH):
            ci = (p + rots[core]) % CH
            cs = slice(ci * PPC * W, (ci + 1) * PPC * W)
            g.sync.dma_start(T.kvs[:, _pairs(ci), 0:W], T.k[:, cs]).then_inc(sem["ldk%d" % ci], 16)
            g.scalar.dma_start(T.kvs[:, _pairs(ci), W:2 * W], T.v[:, cs]).then_inc(sem["ldv%d" % ci], 16)
            if p == HEADN - 1:
                g.sync.dma_start(T.qs[:, :], T.q[:, :]).then_inc(sem.ldq, 16)
                g.scalar.dma_start(T.qland[:, idx, :], T.q[:, idx * W:(idx + 1) * W]).then_inc(sem.ldqo, 16)
    sent = 0
    for waits, trs in calls.get(core, []):
        for name, val in waits:
            g.wait_ge(sem[name], expect[(core, name)] if val is None else val)
        lst = []
        for dst, dap, sap, name, m, e in trs:
            rid, pid = topo.addr(dst)[:2]
            lst.append(RemoteDMATransfer(dst_ids=[DstId(rid=rid, pnc=pid)], dma_engine_mask=m, remote_sem=sem[name],
                                         src=sap, dst=dap))
            sent += e
        g.remote_dma_fused(lst, local_sem=sem.sent)
    for w in mine:
        if w["sink"] is None:
            _worker(g, T, core, w, idx, expect, when)
        else:
            _spare(g, T, core, w, expect)
    if sent:
        g.wait_ge(sem.sent, sent)
    if idx is not None:
        hb = idx // HR
        ca = slice((1 - hb) * HR * W, (2 - hb) * HR * W)
        cb = slice(hb * HR * W, (hb + 1) * HR * W)
        g.scalar.wait_ge(sem.yinA, expect[(core, "yinA")])
        g.scalar.dma_start(T.y[:, ca], T.yland[:, ca]).then_inc(sem.stA, 16)
        g.scalar.wait_ge(sem.stA, 16)
        g.sync.wait_ge(sem.yinB, expect[(core, "yinB")])
        g.sync.wait_ge(sem.own, NHW)
        g.sync.dma_start(T.y[:, cb], T.yland[:, cb]).then_inc(sem.st, 16)
        g.sync.wait_ge(sem.st, 16)
